import numpy as np
import ml_dtypes


def mxq(x, axis, fmt="e4m3"):
    dtype, down = {"e4m3": (ml_dtypes.float8_e4m3fn, 7), "e5m2": (ml_dtypes.float8_e5m2, 14)}[fmt]
    v = np.moveaxis(np.asarray(x, np.float32).astype(ml_dtypes.bfloat16).astype(np.float64), axis, -1)
    blocks = v.reshape(v.shape[:-1] + (-1, 32))
    amax = np.abs(blocks).max(-1, keepdims=True)
    byte = np.maximum(np.where(amax > 0, np.frexp(amax)[1] - 1 + 127, 0) - down, 1)
    scale = np.exp2(byte - 127.0)
    codes = (blocks / scale).astype(np.float32).astype(dtype).astype(np.float64)
    return np.moveaxis((codes * scale).reshape(v.shape), -1, axis)


WIDE = False


def mx_kscale(k):
    if not WIDE:
        return np.ones(k)
    levels = np.array([10, -10, 5, -5, 0])
    if k % 512:
        return np.exp2(np.random.permutation(np.resize(levels, k // 32))).repeat(32)
    a = np.empty((k // 512, 16))
    for p in range(k // 512):
        a[p, :8] = np.random.permutation(np.resize(levels, 8))
        for g in range(8):
            far = levels[np.abs(levels - a[p, g]) >= 10]
            a[p, g + 8] = far[np.random.randint(len(far))]
    return np.exp2(a.ravel()).repeat(32)


BF16 = ml_dtypes.bfloat16


def bf(x):
    return np.asarray(x, np.float32).astype(BF16)


def f64(x):
    return np.asarray(x).astype(np.float64)


E2M1 = np.array([0.0, 0.5, 1.0, 1.5, 2.0, 3.0, 4.0, 6.0, -0.0, -0.5, -1.0, -1.5, -2.0, -3.0, -4.0, -6.0])


def pack_weight(w, fmt):
    k, n = w.shape
    w = f64(bf(w)).reshape(k // 32, 32, n)
    amax = np.abs(w).max(1)
    if fmt == "e4m3":
        byte = np.frexp(amax)[1] - 1 + 127 - 7
    else:
        mant, ex = np.frexp(amax / 6.0)
        byte = np.where(mant > 0.5, ex, ex - 1) + 127
    byte = np.clip(np.where(amax > 0, byte, 1), 1, 254)
    scaled = (w * np.exp2(127.0 - byte)[:, None, :]).reshape(k, n).astype(np.float32)
    by_word = np.ascontiguousarray(scaled.reshape(k // 512, 128, 4, n).transpose(0, 1, 3, 2))
    if fmt == "e4m3":
        words = by_word.astype(ml_dtypes.float8_e4m3fn).view(np.uint8)
    else:
        c = by_word.astype(ml_dtypes.float4_e2m1fn).view(np.uint8) & 0xF
        words = c[..., 0::2] | (c[..., 1::2] << 4)
    return np.ascontiguousarray(words), np.ascontiguousarray(byte.astype(np.uint8).reshape(k // 512, 16, n))


def unpack_weight(words, scales, fmt):
    g, p, n, _ = words.shape
    if fmt == "e4m3":
        vals = np.ascontiguousarray(words).view(ml_dtypes.float8_e4m3fn).astype(np.float64)
    else:
        nib = np.empty((g, p, n, 4), np.uint8)
        nib[..., 0::2] = words & 0xF
        nib[..., 1::2] = words >> 4
        vals = E2M1[nib]
    vals = vals * np.repeat(np.exp2(scales.astype(np.float64) - 127.0), 8, axis=1)[..., None]
    return vals.transpose(0, 1, 3, 2).reshape(g * 512, n)
def pack4(w):
    words, scales = pack_weight(w, "e2m1")
    return words.reshape(words.shape[0], 128, -1), scales


def unpack4(words, scales):
    return unpack_weight(words.reshape(words.shape[0], 128, -1, 2), scales, "e2m1")


N, K, D, F, P = 256, 4, 1024, 1024, 1024


def tanh_derivatives(th):
    d1 = 1.0 - th * th
    d2 = -2.0 * th * d1
    return d1, d2


def draw0():
    s, t = mx_kscale(D), mx_kscale(F)
    x = bf(np.random.standard_normal((N, D)) * s)
    j = bf(np.random.standard_normal((K, N, D)) / np.sqrt(K) * s)
    l = bf(np.random.standard_normal((N, D)) * s)
    w1_words, w1_scales = pack4(np.random.standard_normal((D, F)) / np.sqrt(D) / s[:, None])
    b = bf(0.5 * np.random.standard_normal(F))
    g = bf((1.0 + 0.1 * np.random.standard_normal(F)) * t)
    w2_words, w2_scales = pack4(np.random.standard_normal((F, P)) / np.sqrt(F) / t[:, None])
    return {"x": x,
            "j": j,
            "l": l,
            "w1_words": w1_words,
            "w1_scales": w1_scales,
            "b": b,
            "g": g,
            "w2_words": w2_words,
            "w2_scales": w2_scales}


def core(x, j, l, w1_words, w1_scales, b, g, w2_words, w2_scales):
    gain = f64(g)
    w1q = unpack4(w1_words, w1_scales)
    w2q = unpack4(w2_words, w2_scales)

    a = (mxq(f64(x), 1, "e4m3") @ w1q) + f64(b)
    th = np.tanh(a)

    ja = mxq(f64(j), 2, "e4m3") @ w1q

    la = mxq(f64(l), 1, "e4m3") @ w1q

    d1, d2 = tanh_derivatives(th)

    lh = d1 * la + d2 * np.sum(ja * ja, axis=0)

    lap = mxq(lh * gain, 1, "e4m3") @ w2q

    y = mxq(th * gain, 1, "e4m3") @ w2q
    return lap, y


def e4m3fn_bytes(y):
    return np.clip(np.asarray(y, np.float64), -448.0, 448.0).astype(np.float32).astype(ml_dtypes.float8_e4m3fn).view(np.uint8)


def e4m3fn_values(b):
    return np.asarray(b, np.uint8).view(ml_dtypes.float8_e4m3fn).astype(np.float64)


def setup_inputs():
    d = draw0()
    x0 = np.asarray(d['j']).astype(np.float64)
    s = (np.max(np.abs(x0), axis=(0, 1), keepdims=True) / 448.0).astype(np.float32)
    out = {}
    for k, v in d.items():
        if k == 'j':
            out['j_bytes'] = e4m3fn_bytes(x0 / s.astype(np.float64))
            out['j_scale'] = s
        else:
            out[k] = v
    return out


def reference(x, j_bytes, j_scale, l, w1_words, w1_scales, b, g, w2_words, w2_scales):
    return core(x, e4m3fn_values(j_bytes) * j_scale.astype(np.float64), l, w1_words, w1_scales, b, g, w2_words, w2_scales)

@@ -1,0 +1,468 @@
+from contextlib import ExitStack
+
+import concourse.mybir as mybir
+from concourse.masks import make_identity
+
+N, K, D, F, P_OUT = 256, 4, 1024, 1024, 1024
+FLOPS = 2 * (K + 2) * N * D * F + 2 * 2 * N * F * P_OUT
+
+F32 = mybir.dt.float32
+BF16 = mybir.dt.bfloat16
+I32 = mybir.dt.int32
+U32 = mybir.dt.uint32
+U8 = mybir.dt.uint8
+FP8 = mybir.dt.float8_e4m3fn
+FP8X4 = mybir.dt.float8_e4m3fn_x4
+FP4X4 = mybir.dt.float4_e2m1fn_x4
+ALU = mybir.AluOpType
+ACT = mybir.ActivationFunctionType
+
+P = 128
+PACK = 4
+PASS = P * PACK
+PASSES = D // PASS
+HALVES = N // P
+BANK = 512
+J_TILES = HALVES * K
+
+
+def tile_forwardlaplaciantanhlayer_w4_kernel(
+    tc, x, j_bytes, j_scale, l, w1_words, w1_scales, b, g, w2_words, w2_scales, out_0, out_1
+):
+    nc = tc.nc
+    with ExitStack() as ctx:
+        keep = ctx.enter_context(tc.tile_pool(name="keep", bufs=1))
+        work = ctx.enter_context(tc.tile_pool(name="work", bufs=3))
+        psum = ctx.enter_context(tc.psum_pool(name="psum", bufs=1))
+        ctx.enter_context(tc.manual_schedule())
+
+        ident = keep.tile([P, P], F32, name="ident")
+        warm = keep.tile([P, 8], F32, name="warm")
+        warm_out = keep.tile([P, 8], F32, name="warm_out")
+        scale_col = keep.tile([P, PASSES, PACK], F32, name="scale_col")
+        scale_row = keep.tile([P, D], F32, name="scale_row")
+        b_raw = keep.tile([P, PASSES, PACK], BF16, name="b_raw")
+        g_raw = keep.tile([P, PASSES, PACK], BF16, name="g_raw")
+        bias = keep.tile([P, PASSES, PACK], F32, name="bias")
+        gain = keep.tile([P, PASSES, PACK], F32, name="gain")
+        neg_gain = keep.tile([P, PASSES, PACK], F32, name="neg_gain")
+        w1 = [keep.tile([P, PASSES, 2 * PASS], U8, name="w1_%d" % c, align_bytes=64) for c in range(2)]
+        s1 = keep.tile([P, PASSES, F], U8, name="s1", align_bytes=64)
+        w2 = keep.tile([P, PASSES, 2 * P_OUT], U8, name="w2", align_bytes=64)
+        s2 = keep.tile([P, PASSES, P_OUT], U8, name="s2", align_bytes=64)
+        w1_by_slot = [keep.tile([P, PASSES, 2 * PASS], U8, name="w1_by_slot%d" % c, align_bytes=64) for c in range(2)]
+        s1_by_slot = [keep.tile([P, PASSES, PASS], U8, name="s1_by_slot%d" % c, align_bytes=64) for c in range(2)]
+        rows_bf = [keep.tile([P, HALVES, D], BF16, name="rows_bf%d" % i) for i in range(2)]
+        j_raw = [keep.tile([P, D], U8, name="j_raw%d" % s) for s in range(J_TILES)]
+        xl_turned = [keep.tile([P, 2 * N * PACK], BF16, name="xl_turned%d" % q, align_bytes=64) for q in range(PASSES)]
+        xl_codes = [keep.tile([P, 2 * N], U32, name="xl_codes%d" % q, align_bytes=64) for q in range(PASSES)]
+        xl_scales = [keep.tile([P, 2 * N], U8, name="xl_scales%d" % q, align_bytes=64) for q in range(PASSES)]
+        th = [keep.tile([P, PACK, N], F32, name="th%d" % c) for c in range(2)]
+        th_gain = [keep.tile([P, PACK, N], F32, name="th_gain%d" % c) for c in range(2)]
+        la_gain = [keep.tile([P, PACK, N], F32, name="la_gain%d" % c) for c in range(2)]
+        th_sq = [[keep.tile([P, P, PACK], F32, name="th_sq%d_%d" % (h, c)) for c in range(2)] for h in range(HALVES)]
+        y_codes = [keep.tile([P, N], U32, name="y_codes%d" % c, align_bytes=64) for c in range(2)]
+        y_scales = [keep.tile([P, N], U8, name="y_scales%d" % c, align_bytes=64) for c in range(2)]
+        lap_codes = [[keep.tile([P, P], U32, name="lap_codes%d_%d" % (h, c), align_bytes=64) for c in range(2)] for h in range(HALVES)]
+        lap_scales = [[keep.tile([P, P], U8, name="lap_scales%d_%d" % (h, c), align_bytes=64) for c in range(2)] for h in range(HALVES)]
+
+        live = {}
+
+        def load_words(dst, src):
+            nc.sync.dma_start(out=dst[:].bitcast(I32), in_=src.rearrange("q p n -> p q n").bitcast(I32))
+
+        def load_scales(dst, src):
+            for quad in range(4):
+                nc.sync.dma_start(
+                    out=dst[32 * quad : 32 * quad + 4].bitcast(I32),
+                    in_=src[:, 4 * quad : 4 * quad + 4, :].rearrange("q r n -> r q n").bitcast(I32),
+                )
+
+        def load_j(s):
+            h, k = divmod(s, K)
+            nc.sync.dma_start(out=j_raw[s][:], in_=j_bytes[k, h * P : (h + 1) * P, :])
+
+        def spread_scale(q):
+            bank = psum.tile([P, PACK, P], F32, name="turn", bufs=2)
+            for t in range(PACK):
+                nc.tensor.transpose(bank[:, t, :], scale_col[:, q, t : t + 1].to_broadcast([P, P]), ident[:])
+            nc.scalar.copy(
+                out=scale_row[:, q * PASS : (q + 1) * PASS].rearrange("p (n t) -> p n t", t=PACK),
+                in_=bank[:].rearrange("p t n -> p n t"),
+            )
+
+        def turn_xl(i, q):
+            bank = psum.tile([P, 2, N], F32, name="turn", bufs=2)
+            words = rows_bf[i][:].bitcast(F32)
+            for h in range(HALVES):
+                for u in range(2):
+                    nc.tensor.transpose(
+                        bank[:, u, h * P : (h + 1) * P], words[:, h, 256 * q + u : 256 * (q + 1) : 2], ident[:]
+                    )
+            live["xl", i, q] = bank
+
+        def empty_xl(i, q):
+            dst = xl_turned[q][:, i * N * PACK : (i + 1) * N * PACK].bitcast(F32)
+            nc.scalar.copy(out=dst.rearrange("p (n u) -> p n u", u=2), in_=live["xl", i, q][:].rearrange("p u n -> p n u"))
+
+        def quantize_xl(q):
+            nc.vector.quantize_mx(out=xl_codes[q][:].bitcast(FP8X4), scales=xl_scales[q][:], in_=xl_turned[q][:])
+
+        def order_words(c, q):
+            nc.vector.tensor_copy(
+                out=w1_by_slot[c][:, q, :].rearrange("p (t a m e) -> p a t m e", t=PACK, m=8, e=2),
+                in_=w1[c][:, q, :].rearrange("p (a m t e) -> p a t m e", t=PACK, m=8, e=2),
+            )
+
+        def order_scales(c):
+            nc.vector.tensor_copy(
+                out=s1_by_slot[c][:].rearrange("p q (t a m) -> p q a t m", t=PACK, m=16),
+                in_=s1[:, :, PASS * c : PASS * (c + 1)].rearrange("p q (a m t) -> p q a t m", t=PACK, m=16),
+            )
+
+        def widen(s, parts=1):
+            wide = work.tile([P, D], BF16, name="wide")
+            for part in range(parts):
+                cols = slice(part * D // parts, (part + 1) * D // parts)
+                nc.vector.tensor_tensor(out=wide[:, cols], in0=j_raw[s][:, cols].bitcast(FP8), in1=scale_row[:, cols], op=ALU.mult)
+            live["wide", s] = wide
+
+        def turn_j(s):
+            bank = psum.tile([P, PASSES, 2, P], F32, name="turn", bufs=2)
+            words = live["wide", s][:].bitcast(F32)
+            for q in range(PASSES):
+                for u in range(2):
+                    nc.tensor.transpose(bank[:, q, u, :], words[:, 256 * q + u : 256 * (q + 1) : 2], ident[:])
+            live["turn", s] = bank
+
+        def empty_j(s):
+            turned = work.tile([P, D], BF16, name="turned", align_bytes=64)
+            nc.scalar.copy(
+                out=turned[:].bitcast(F32).rearrange("p (q n u) -> p q n u", q=PASSES, u=2),
+                in_=live["turn", s][:].rearrange("p q u n -> p q n u"),
+            )
+            live["turned", s] = turned
+
+        def quantize_j(s):
+            codes = work.tile([P, PASSES * P], U32, name="j_codes", bufs=J_TILES, align_bytes=64)
+            scales = work.tile([P, PASSES * P], U8, name="j_scales", bufs=J_TILES, align_bytes=64)
+            nc.vector.quantize_mx(out=codes[:].bitcast(FP8X4), scales=scales[:], in_=live["turned", s][:])
+            live["jq", s] = (codes, scales)
+
+        def multiply_j(s, c):
+            codes, scales = live["jq", s]
+            bank = psum.tile([P, BANK], F32, name="acc", bufs=4)
+            for q in range(PASSES):
+                nc.tensor.matmul_mx(
+                    out=bank[:],
+                    lhsT=codes[:, q * P : (q + 1) * P].bitcast(FP8X4),
+                    lhsT_scale=scales[:, q * P : (q + 1) * P],
+                    rhs=w1[c][:, q, :].bitcast(FP4X4),
+                    rhs_scale=s1[:, q, PASS * c : PASS * (c + 1)],
+                    start=(q == 0),
+                    stop=(q == PASSES - 1),
+                )
+            live["ja", s, c] = bank
+
+        def square(s, c):
+            sq = work.tile([P, PACK, P], F32, name="sq", bufs=6)
+            nc.scalar.activation(out=sq[:], in_=live["ja", s, c][:].rearrange("p (m t) -> p t m", t=PACK), func=ACT.Square)
+            live["sq", s, c] = sq
+
+        def fold(s, c):
+            h, k = divmod(s, K)
+            if k == 0:
+                live["sum", h, c] = psum.tile([P, PACK, P], F32, name="sum%d" % c)
+            bank = live["sum", h, c]
+            for t in range(PACK):
+                nc.tensor.matmul(
+                    bank[:, t, :],
+                    lhsT=live["sq", s, c][:, t, :],
+                    rhs=ident[:],
+                    start=(k == 0 and t == 0),
+                    stop=(k == K - 1 and t == PACK - 1),
+                    is_transpose=True,
+                )
+
+        def multiply_xl(c, t):
+            bank = psum.tile([P, 2, N], F32, name="acc", bufs=4)
+            for q in range(PASSES):
+                nc.tensor.matmul_mx(
+                    out=bank[:].rearrange("p i n -> p (i n)"),
+                    lhsT=w1_by_slot[c][:, q, 2 * P * t : 2 * P * (t + 1)].bitcast(FP4X4),
+                    lhsT_scale=s1_by_slot[c][:, q, P * t : P * (t + 1)],
+                    rhs=xl_codes[q][:].bitcast(FP8X4),
+                    rhs_scale=xl_scales[q][:],
+                    start=(q == 0),
+                    stop=(q == PASSES - 1),
+                )
+            live["al", c, t] = bank
+
+        def activate(c, t):
+            bank = live["al", c, t]
+            nc.scalar.activation(out=th[c][:, t, :], in_=bank[:, 0, :], func=ACT.Tanh, bias=bias[:, c, t : t + 1])
+            nc.scalar.activation(out=la_gain[c][:, t, :], in_=bank[:, 1, :], func=ACT.Copy, scale=neg_gain[:, c, t : t + 1])
+
+        def apply_gain(c, t):
+            nc.vector.tensor_scalar(
+                out=th_gain[c][:, t, :], in0=th[c][:, t, :], scalar1=gain[:, c, t : t + 1], scalar2=None, op0=ALU.mult
+            )
+
+        def square_th(h, c):
+            nc.scalar.activation(
+                out=th_sq[h][c][:], in_=th[c][:, :, h * P : (h + 1) * P].rearrange("p t n -> p n t"), func=ACT.Square
+            )
+
+        def round_y(c):
+            y_in = work.tile([P, N, PACK], BF16, name="y_in", bufs=2, align_bytes=64)
+            nc.vector.tensor_copy(out=y_in[:], in_=th_gain[c][:].rearrange("p t n -> p n t"))
+            live["y_in", c] = y_in
+
+        def quantize_y(c):
+            nc.vector.quantize_mx(
+                out=y_codes[c][:].bitcast(FP8X4), scales=y_scales[c][:], in_=live["y_in", c][:].rearrange("p n t -> p (n t)")
+            )
+
+        def lap_product(h, c):
+            u = work.tile([P, PACK, P], F32, name="lap_u", bufs=2)
+            nc.vector.scalar_tensor_tensor(
+                out=u[:], in0=live["sum", h, c][:], scalar=2.0, in1=th_gain[c][:, :, h * P : (h + 1) * P],
+                op0=ALU.mult, op1=ALU.mult,
+            )
+            live["u", h, c] = u
+
+        def lap_sum(h, c):
+            v = work.tile([P, PACK, P], F32, name="lap_v", bufs=2)
+            nc.vector.tensor_tensor(out=v[:], in0=live["u", h, c][:], in1=la_gain[c][:, :, h * P : (h + 1) * P], op=ALU.add)
+            live["v", h, c] = v
+
+        def lap_round(h, c):
+            lap_in = work.tile([P, P, PACK], BF16, name="lap_in", bufs=2, align_bytes=64)
+            nc.vector.scalar_tensor_tensor(
+                out=lap_in[:], in0=th_sq[h][c][:], scalar=-1.0, in1=live["v", h, c][:].rearrange("p t n -> p n t"),
+                op0=ALU.add, op1=ALU.mult,
+            )
+            live["lap_in", h, c] = lap_in
+
+        def quantize_lap(h, c):
+            nc.vector.quantize_mx(
+                out=lap_codes[h][c][:].bitcast(FP8X4),
+                scales=lap_scales[h][c][:],
+                in_=live["lap_in", h, c][:].rearrange("p n t -> p (n t)"),
+            )
+
+        def lap_factors(h, c):
+            tokens = slice(h * P, (h + 1) * P)
+            for name, src in (("slope", th_gain), ("base", la_gain)):
+                dst = work.tile([P, P, PACK], F32, name=name, bufs=1)
+                nc.vector.scalar_tensor_tensor(
+                    out=dst[:], in0=th_sq[h][c][:], scalar=-1.0, in1=src[c][:, :, tokens].rearrange("p t n -> p n t"),
+                    op0=ALU.add, op1=ALU.mult,
+                )
+                live[name] = dst
+
+        def lap_last(h, c):
+            term = work.tile([P, P, PACK], F32, name="term", bufs=1)
+            lap_in = work.tile([P, P, PACK], BF16, name="lap_in", bufs=2, align_bytes=64)
+            halves = [slice(0, P // 2), slice(P // 2, P)]
+            for part in halves:
+                nc.vector.scalar_tensor_tensor(
+                    out=term[:, part, :], in0=live["sum", h, c][:, :, part].rearrange("p t n -> p n t"), scalar=2.0,
+                    in1=live["slope"][:, part, :], op0=ALU.mult, op1=ALU.mult,
+                )
+            for part in halves:
+                nc.vector.tensor_tensor(out=lap_in[:, part, :], in0=term[:, part, :], in1=live["base"][:, part, :], op=ALU.add)
+            live["lap_in", h, c] = lap_in
+
+        def multiply_out(key, codes, scales, c):
+            for n in range(2):
+                if c == 0:
+                    live[key, n] = psum.tile([P, BANK], F32, name="acc", bufs=4)
+                nc.tensor.matmul_mx(
+                    out=live[key, n][:],
+                    lhsT=codes.bitcast(FP8X4),
+                    lhsT_scale=scales,
+                    rhs=w2[:, c, 2 * BANK * n : 2 * BANK * (n + 1)].bitcast(FP4X4),
+                    rhs_scale=s2[:, c, BANK * n : BANK * (n + 1)],
+                    start=(c == 0),
+                    stop=(c == 1),
+                )
+
+        def multiply_y(h, c):
+            multiply_out(("y", h), y_codes[c][:, h * P : (h + 1) * P], y_scales[c][:, h * P : (h + 1) * P], c)
+
+        def multiply_lap(h, c):
+            multiply_out(("lap", h), lap_codes[h][c][:], lap_scales[h][c][:], c)
+
+        def store(key, dst, h, n, on_vector):
+            result = work.tile([P, BANK], F32, name="result", bufs=8)
+            if on_vector:
+                nc.vector.tensor_copy(out=result[:], in_=live[(key, h), n][:])
+            else:
+                nc.scalar.copy(out=result[:], in_=live[(key, h), n][:])
+            nc.sync.dma_start(out=dst[h * P : (h + 1) * P, n * BANK : (n + 1) * BANK], in_=result[:])
+
+        nc.sync.dma_start(out=scale_col[:], in_=j_scale.rearrange("a o (q p t) -> p (a o q) t", p=P, t=PACK))
+        nc.vector.memset(s1[:].bitcast(I32), 0)
+        nc.vector.memset(warm[:], 0.0)
+        nc.vector.memset(s2[:].bitcast(I32), 0)
+        make_identity(nc, ident[:])
+        nc.scalar.activation(out=warm_out[:], in_=warm[:], func=ACT.Tanh)
+        load_j(0)
+        load_scales(s1, w1_scales)
+        load_words(w1[0], w1_words[:, :, : 2 * PASS])
+        nc.sync.dma_start(out=rows_bf[0][:], in_=x.rearrange("(h p) d -> p h d", p=P))
+        load_j(1)
+        nc.sync.dma_start(out=rows_bf[1][:], in_=l.rearrange("(h p) d -> p h d", p=P))
+        load_words(w1[1], w1_words[:, :, 2 * PASS :])
+        load_j(2)
+        nc.sync.dma_start(out=b_raw[:], in_=b.rearrange("(q p t) -> p q t", p=P, t=PACK))
+        nc.sync.dma_start(out=g_raw[:], in_=g.rearrange("(q p t) -> p q t", p=P, t=PACK))
+        for s in range(3, J_TILES):
+            load_j(s)
+        load_scales(s2, w2_scales)
+        load_words(w2, w2_words)
+
+        def al(i):
+            c, t = divmod(i, PACK)
+            multiply_xl(c, t)
+            activate(c, t)
+
+        def jm(s, c):
+            multiply_j(s, c)
+            square(s, c)
+
+        def gains(c):
+            for t in range(PACK):
+                apply_gain(c, t)
+
+        def turn(s):
+            turn_j(s)
+            empty_j(s)
+
+        for q in range(PASSES):
+            spread_scale(q)
+        order_scales(0)
+        widen(0, 2)
+        order_words(0, 0)
+        turn(0)
+        widen(1)
+        turn_xl(0, 0)
+        empty_xl(0, 0)
+        quantize_j(0)
+        turn_xl(0, 1)
+        empty_xl(0, 1)
+        jm(0, 0)
+        turn(1)
+        widen(2)
+        turn_xl(1, 0)
+        empty_xl(1, 0)
+        jm(0, 1)
+        quantize_j(1)
+        order_words(0, 1)
+        turn_xl(1, 1)
+        empty_xl(1, 1)
+        turn(2)
+        nc.vector.tensor_copy(out=bias[:], in_=b_raw[:])
+        nc.vector.tensor_copy(out=gain[:], in_=g_raw[:])
+        nc.vector.tensor_scalar(out=neg_gain[:], in0=g_raw[:], scalar1=-1.0, scalar2=None, op0=ALU.mult)
+        quantize_xl(0)
+        widen(3)
+        jm(1, 0)
+        jm(1, 1)
+        quantize_xl(1)
+        quantize_j(2)
+        turn(3)
+        fold(0, 0)
+        fold(0, 1)
+        widen(4)
+        order_scales(1)
+        quantize_j(3)
+        al(0)
+        jm(2, 0)
+        al(1)
+        jm(2, 1)
+        turn(4)
+        fold(1, 0)
+        fold(1, 1)
+        widen(5)
+        order_words(1, 0)
+        quantize_j(4)
+        order_words(1, 1)
+        al(2)
+        jm(3, 0)
+        al(3)
+        jm(3, 1)
+        turn(5)
+        fold(2, 0)
+        fold(2, 1)
+        widen(6)
+        gains(0)
+        quantize_j(5)
+        al(4)
+        jm(4, 0)
+        al(5)
+        round_y(0)
+        turn(6)
+        fold(3, 0)
+        fold(3, 1)
+        widen(7)
+        quantize_j(6)
+        lap_product(0, 0)
+        quantize_y(0)
+        al(6)
+        jm(5, 0)
+        al(7)
+        square_th(0, 0)
+        lap_sum(0, 0)
+        turn(7)
+        fold(4, 0)
+        fold(5, 0)
+        gains(1)
+        quantize_j(7)
+        lap_product(0, 1)
+        jm(6, 0)
+        jm(4, 1)
+        square_th(0, 1)
+        round_y(1)
+        lap_round(0, 0)
+        lap_sum(0, 1)
+        quantize_y(1)
+        jm(7, 0)
+        jm(5, 1)
+        square_th(1, 0)
+        fold(6, 0)
+        fold(4, 1)
+        fold(7, 0)
+        quantize_lap(0, 0)
+        lap_round(0, 1)
+        lap_product(1, 0)
+        quantize_lap(0, 1)
+        jm(6, 1)
+        square_th(1, 1)
+        jm(7, 1)
+        lap_sum(1, 0)
+        multiply_y(0, 0)
+        multiply_y(0, 1)
+        lap_factors(1, 1)
+        fold(5, 1)
+        fold(6, 1)
+        fold(7, 1)
+        lap_round(1, 0)
+        for n in range(2):
+            store("y", out_1, 0, n, False)
+        multiply_y(1, 0)
+        multiply_y(1, 1)
+        lap_last(1, 1)
+        quantize_lap(1, 0)
+        quantize_lap(1, 1)
+        for n in range(2):
+            store("y", out_1, 1, n, False)
+        multiply_lap(0, 0)
+        multiply_lap(0, 1)
+        for n in range(2):
+            store("lap", out_0, 0, n, n == 0)
+        multiply_lap(1, 0)
+        multiply_lap(1, 1)
+        for n in range(2):
+            store("lap", out_0, 1, n, n == 0)

@@ -18,12 +18,18 @@ ALU = mybir.AluOpType
 ACT = mybir.ActivationFunctionType
 
 P = 128
-PACK = 4
-PASS = P * PACK
+SLOTS = 4
+PASS = P * SLOTS
 PASSES = D // PASS
+GROUPS = F // PASS
 HALVES = N // P
 BANK = 512
+COLS = P_OUT // BANK
 J_TILES = HALVES * K
+PASS_WORDS = PASS // 2
+W4 = 2
+LINE = 16
+TURN_BANKS, PRODUCT_BANKS = 2, 4
 
 
 def tile_forwardlaplaciantanhlayer_w4_kernel(
@@ -32,41 +38,50 @@ def tile_forwardlaplaciantanhlayer_w4_kernel(
     nc = tc.nc
     with ExitStack() as ctx:
         keep = ctx.enter_context(tc.tile_pool(name="keep", bufs=1))
-        work = ctx.enter_context(tc.tile_pool(name="work", bufs=3))
+        work = ctx.enter_context(tc.tile_pool(name="work", bufs=2))
         psum = ctx.enter_context(tc.psum_pool(name="psum", bufs=1))
         ctx.enter_context(tc.manual_schedule())
 
-        ident = keep.tile([P, P], F32, name="ident")
-        warm = keep.tile([P, 8], F32, name="warm")
-        warm_out = keep.tile([P, 8], F32, name="warm_out")
-        scale_col = keep.tile([P, PASSES, PACK], F32, name="scale_col")
-        scale_row = keep.tile([P, D], F32, name="scale_row")
-        b_raw = keep.tile([P, PASSES, PACK], BF16, name="b_raw")
-        g_raw = keep.tile([P, PASSES, PACK], BF16, name="g_raw")
-        bias = keep.tile([P, PASSES, PACK], F32, name="bias")
-        gain = keep.tile([P, PASSES, PACK], F32, name="gain")
-        neg_gain = keep.tile([P, PASSES, PACK], F32, name="neg_gain")
-        w1 = [keep.tile([P, PASSES, 2 * PASS], U8, name="w1_%d" % c, align_bytes=64) for c in range(2)]
-        s1 = keep.tile([P, PASSES, F], U8, name="s1", align_bytes=64)
-        w2 = keep.tile([P, PASSES, 2 * P_OUT], U8, name="w2", align_bytes=64)
-        s2 = keep.tile([P, PASSES, P_OUT], U8, name="s2", align_bytes=64)
-        w1_by_slot = [keep.tile([P, PASSES, 2 * PASS], U8, name="w1_by_slot%d" % c, align_bytes=64) for c in range(2)]
-        s1_by_slot = [keep.tile([P, PASSES, PASS], U8, name="s1_by_slot%d" % c, align_bytes=64) for c in range(2)]
-        rows_bf = [keep.tile([P, HALVES, D], BF16, name="rows_bf%d" % i) for i in range(2)]
-        j_raw = [keep.tile([P, D], U8, name="j_raw%d" % s) for s in range(J_TILES)]
-        xl_turned = [keep.tile([P, 2 * N * PACK], BF16, name="xl_turned%d" % q, align_bytes=64) for q in range(PASSES)]
-        xl_codes = [keep.tile([P, 2 * N], U32, name="xl_codes%d" % q, align_bytes=64) for q in range(PASSES)]
-        xl_scales = [keep.tile([P, 2 * N], U8, name="xl_scales%d" % q, align_bytes=64) for q in range(PASSES)]
-        th = [keep.tile([P, PACK, N], F32, name="th%d" % c) for c in range(2)]
-        th_gain = [keep.tile([P, PACK, N], F32, name="th_gain%d" % c) for c in range(2)]
-        la_gain = [keep.tile([P, PACK, N], F32, name="la_gain%d" % c) for c in range(2)]
-        th_sq = [[keep.tile([P, P, PACK], F32, name="th_sq%d_%d" % (h, c)) for c in range(2)] for h in range(HALVES)]
-        y_codes = [keep.tile([P, N], U32, name="y_codes%d" % c, align_bytes=64) for c in range(2)]
-        y_scales = [keep.tile([P, N], U8, name="y_scales%d" % c, align_bytes=64) for c in range(2)]
-        lap_codes = [[keep.tile([P, P], U32, name="lap_codes%d_%d" % (h, c), align_bytes=64) for c in range(2)] for h in range(HALVES)]
-        lap_scales = [[keep.tile([P, P], U8, name="lap_scales%d_%d" % (h, c), align_bytes=64) for c in range(2)] for h in range(HALVES)]
+        def kept(name, shape, dtype):
+            return keep.tile(shape, dtype, name=name, align_bytes=64)
+
+        def per_group(name, shape, dtype):
+            return [kept("%s%d" % (name, c), shape, dtype) for c in range(GROUPS)]
+
+        ident = kept("ident", [P, P], F32)
+        table_in = kept("table_in", [P, 8], F32)
+        table_out = kept("table_out", [P, 8], F32)
+        scale_col = kept("scale_col", [P, PASSES, SLOTS], F32)
+        scale_row = kept("scale_row", [P, D], F32)
+        bias = kept("bias", [P, GROUPS, SLOTS], BF16)
+        gain = kept("gain", [P, GROUPS, SLOTS], BF16)
+        neg_gain = kept("neg_gain", [P, GROUPS, SLOTS], F32)
+        w1 = per_group("w1_", [P, PASSES, W4 * PASS], U8)
+        s1 = kept("s1", [P, PASSES, F], U8)
+        w2 = kept("w2", [P, GROUPS, W4 * P_OUT], U8)
+        s2 = kept("s2", [P, GROUPS, P_OUT], U8)
+        w1_by_slot = per_group("w1_by_slot", [P, PASSES, W4 * PASS], U8)
+        s1_by_slot = per_group("s1_by_slot", [P, PASSES, PASS], U8)
+        xl_rows = [kept("xl_rows%d" % i, [P, HALVES, D], BF16) for i in range(2)]
+        j_rows = [kept("j_rows%d" % s, [P, D], U8) for s in range(J_TILES)]
+        xl_turned = [kept("xl_turned%d" % q, [P, 2 * N * SLOTS], BF16) for q in range(PASSES)]
+        xl_codes = [kept("xl_codes%d" % q, [P, 2 * N], U32) for q in range(PASSES)]
+        xl_scales = [kept("xl_scales%d" % q, [P, 2 * N], U8) for q in range(PASSES)]
+        j_codes = [kept("j_codes%d" % s, [P, PASSES * P], U32) for s in range(J_TILES)]
+        j_scales = [kept("j_scales%d" % s, [P, PASSES * P], U8) for s in range(J_TILES)]
+        th = per_group("th", [P, SLOTS, N], F32)
+        th_gain = per_group("th_gain", [P, SLOTS, N], F32)
+        la_gain = per_group("la_gain", [P, SLOTS, N], F32)
+        th_sq = [per_group("th_sq%d_" % h, [P, P, SLOTS], F32) for h in range(HALVES)]
+        y_codes = per_group("y_codes", [P, N], U32)
+        y_scales = per_group("y_scales", [P, N], U8)
+        lap_codes = [per_group("lap_codes%d_" % h, [P, P], U32) for h in range(HALVES)]
+        lap_scales = [per_group("lap_scales%d_" % h, [P, P], U8) for h in range(HALVES)]
 
         live = {}
+
+        def tokens(h):
+            return slice(h * P, (h + 1) * P)
 
         def load_words(dst, src):
             nc.sync.dma_start(out=dst[:].bitcast(I32), in_=src.rearrange("q p n -> p q n").bitcast(I32))
@@ -80,168 +95,202 @@ def tile_forwardlaplaciantanhlayer_w4_kernel(
 
         def load_j(s):
             h, k = divmod(s, K)
-            nc.sync.dma_start(out=j_raw[s][:], in_=j_bytes[k, h * P : (h + 1) * P, :])
+            nc.sync.dma_start(out=j_rows[s][:], in_=j_bytes[k, tokens(h), :])
 
         def spread_scale(q):
-            bank = psum.tile([P, PACK, P], F32, name="turn", bufs=2)
-            for t in range(PACK):
+            bank = psum.tile([P, SLOTS, P], F32, name="sum%d" % q)
+            for t in range(SLOTS):
                 nc.tensor.transpose(bank[:, t, :], scale_col[:, q, t : t + 1].to_broadcast([P, P]), ident[:])
             nc.scalar.copy(
-                out=scale_row[:, q * PASS : (q + 1) * PASS].rearrange("p (n t) -> p n t", t=PACK),
+                out=scale_row[:, q * PASS : (q + 1) * PASS].rearrange("p (n t) -> p n t", t=SLOTS),
                 in_=bank[:].rearrange("p t n -> p n t"),
             )
 
+        def every_second_word(q, u):
+            return slice(PASS_WORDS * q + u, PASS_WORDS * (q + 1), 2)
+
         def turn_xl(i, q):
-            bank = psum.tile([P, 2, N], F32, name="turn", bufs=2)
-            words = rows_bf[i][:].bitcast(F32)
+            bank = psum.tile([P, 2, N], F32, name="turn", bufs=TURN_BANKS)
+            words = xl_rows[i][:].bitcast(F32)
             for h in range(HALVES):
                 for u in range(2):
-                    nc.tensor.transpose(
-                        bank[:, u, h * P : (h + 1) * P], words[:, h, 256 * q + u : 256 * (q + 1) : 2], ident[:]
-                    )
-            live["xl", i, q] = bank
-
-        def empty_xl(i, q):
-            dst = xl_turned[q][:, i * N * PACK : (i + 1) * N * PACK].bitcast(F32)
-            nc.scalar.copy(out=dst.rearrange("p (n u) -> p n u", u=2), in_=live["xl", i, q][:].rearrange("p u n -> p n u"))
+                    nc.tensor.transpose(bank[:, u, tokens(h)], words[:, h, every_second_word(q, u)], ident[:])
+            dst = xl_turned[q][:, i * N * SLOTS : (i + 1) * N * SLOTS].bitcast(F32)
+            nc.scalar.copy(out=dst.rearrange("p (n u) -> p n u", u=2), in_=bank[:].rearrange("p u n -> p n u"))
 
         def quantize_xl(q):
             nc.vector.quantize_mx(out=xl_codes[q][:].bitcast(FP8X4), scales=xl_scales[q][:], in_=xl_turned[q][:])
 
         def order_words(c, q):
             nc.vector.tensor_copy(
-                out=w1_by_slot[c][:, q, :].rearrange("p (t a m e) -> p a t m e", t=PACK, m=8, e=2),
-                in_=w1[c][:, q, :].rearrange("p (a m t e) -> p a t m e", t=PACK, m=8, e=2),
+                out=w1_by_slot[c][:, q, :].rearrange("p (t a m e) -> p a t m e", t=SLOTS, m=LINE // W4, e=W4),
+                in_=w1[c][:, q, :].rearrange("p (a m t e) -> p a t m e", t=SLOTS, m=LINE // W4, e=W4),
             )
 
         def order_scales(c):
             nc.vector.tensor_copy(
-                out=s1_by_slot[c][:].rearrange("p q (t a m) -> p q a t m", t=PACK, m=16),
-                in_=s1[:, :, PASS * c : PASS * (c + 1)].rearrange("p q (a m t) -> p q a t m", t=PACK, m=16),
+                out=s1_by_slot[c][:].rearrange("p q (t a m) -> p q a t m", t=SLOTS, m=LINE),
+                in_=s1[:, :, PASS * c : PASS * (c + 1)].rearrange("p q (a m t) -> p q a t m", t=SLOTS, m=LINE),
             )
 
         def widen(s, parts=1):
-            wide = work.tile([P, D], BF16, name="wide")
+            wide = work.tile([P, D], BF16, name="wide", bufs=3)
             for part in range(parts):
                 cols = slice(part * D // parts, (part + 1) * D // parts)
-                nc.vector.tensor_tensor(out=wide[:, cols], in0=j_raw[s][:, cols].bitcast(FP8), in1=scale_row[:, cols], op=ALU.mult)
+                nc.vector.tensor_tensor(
+                    out=wide[:, cols], in0=j_rows[s][:, cols].bitcast(FP8), in1=scale_row[:, cols], op=ALU.mult
+                )
             live["wide", s] = wide
 
         def turn_j(s):
-            bank = psum.tile([P, PASSES, 2, P], F32, name="turn", bufs=2)
+            bank = psum.tile([P, PASSES, 2, P], F32, name="turn", bufs=TURN_BANKS)
             words = live["wide", s][:].bitcast(F32)
             for q in range(PASSES):
                 for u in range(2):
-                    nc.tensor.transpose(bank[:, q, u, :], words[:, 256 * q + u : 256 * (q + 1) : 2], ident[:])
-            live["turn", s] = bank
-
-        def empty_j(s):
-            turned = work.tile([P, D], BF16, name="turned", align_bytes=64)
+                    nc.tensor.transpose(bank[:, q, u, :], words[:, every_second_word(q, u)], ident[:])
+            turned = work.tile([P, D], BF16, name="turned", bufs=3, align_bytes=64)
             nc.scalar.copy(
                 out=turned[:].bitcast(F32).rearrange("p (q n u) -> p q n u", q=PASSES, u=2),
-                in_=live["turn", s][:].rearrange("p q u n -> p q n u"),
+                in_=bank[:].rearrange("p q u n -> p q n u"),
             )
             live["turned", s] = turned
 
         def quantize_j(s):
-            codes = work.tile([P, PASSES * P], U32, name="j_codes", bufs=J_TILES, align_bytes=64)
-            scales = work.tile([P, PASSES * P], U8, name="j_scales", bufs=J_TILES, align_bytes=64)
-            nc.vector.quantize_mx(out=codes[:].bitcast(FP8X4), scales=scales[:], in_=live["turned", s][:])
-            live["jq", s] = (codes, scales)
+            nc.vector.quantize_mx(out=j_codes[s][:].bitcast(FP8X4), scales=j_scales[s][:], in_=live["turned", s][:])
 
-        def multiply_j(s, c):
-            codes, scales = live["jq", s]
-            bank = psum.tile([P, BANK], F32, name="acc", bufs=4)
+        def product_j(s, c):
+            bank = psum.tile([P, BANK], F32, name="product", bufs=PRODUCT_BANKS)
             for q in range(PASSES):
                 nc.tensor.matmul_mx(
                     out=bank[:],
-                    lhsT=codes[:, q * P : (q + 1) * P].bitcast(FP8X4),
-                    lhsT_scale=scales[:, q * P : (q + 1) * P],
+                    lhsT=j_codes[s][:, q * P : (q + 1) * P].bitcast(FP8X4),
+                    lhsT_scale=j_scales[s][:, q * P : (q + 1) * P],
                     rhs=w1[c][:, q, :].bitcast(FP4X4),
                     rhs_scale=s1[:, q, PASS * c : PASS * (c + 1)],
                     start=(q == 0),
                     stop=(q == PASSES - 1),
                 )
-            live["ja", s, c] = bank
+            squares = work.tile([P, SLOTS, P], F32, name="squares", bufs=6)
+            nc.scalar.activation(out=squares[:], in_=bank[:].rearrange("p (m t) -> p t m", t=SLOTS), func=ACT.Square)
+            live["squares", s, c] = squares
 
-        def square(s, c):
-            sq = work.tile([P, PACK, P], F32, name="sq", bufs=6)
-            nc.scalar.activation(out=sq[:], in_=live["ja", s, c][:].rearrange("p (m t) -> p t m", t=PACK), func=ACT.Square)
-            live["sq", s, c] = sq
+        def add_pair(s, c):
+            pair = work.tile([P, SLOTS, P], F32, name="pair")
+            nc.vector.tensor_tensor(
+                out=pair[:], in0=live["squares", s - 1, c][:], in1=live["squares", s, c][:], op=ALU.add
+            )
+            live["squares", s, c] = pair
 
-        def fold(s, c):
+        def fold(s, c, opens=False):
             h, k = divmod(s, K)
-            if k == 0:
-                live["sum", h, c] = psum.tile([P, PACK, P], F32, name="sum%d" % c)
-            bank = live["sum", h, c]
-            for t in range(PACK):
+            if opens:
+                live["sum", h, c] = psum.tile([P, SLOTS, P], F32, name="sum%d" % c)
+            for t in range(SLOTS):
                 nc.tensor.matmul(
-                    bank[:, t, :],
-                    lhsT=live["sq", s, c][:, t, :],
+                    live["sum", h, c][:, t, :],
+                    lhsT=live["squares", s, c][:, t, :],
                     rhs=ident[:],
-                    start=(k == 0 and t == 0),
-                    stop=(k == K - 1 and t == PACK - 1),
+                    start=(opens and t == 0),
+                    stop=(k == K - 1 and t == SLOTS - 1),
                     is_transpose=True,
                 )
 
-        def multiply_xl(c, t):
-            bank = psum.tile([P, 2, N], F32, name="acc", bufs=4)
+        def product_xl(c, t):
+            bank = psum.tile([P, 2, N], F32, name="product", bufs=PRODUCT_BANKS)
             for q in range(PASSES):
                 nc.tensor.matmul_mx(
                     out=bank[:].rearrange("p i n -> p (i n)"),
-                    lhsT=w1_by_slot[c][:, q, 2 * P * t : 2 * P * (t + 1)].bitcast(FP4X4),
+                    lhsT=w1_by_slot[c][:, q, W4 * P * t : W4 * P * (t + 1)].bitcast(FP4X4),
                     lhsT_scale=s1_by_slot[c][:, q, P * t : P * (t + 1)],
                     rhs=xl_codes[q][:].bitcast(FP8X4),
                     rhs_scale=xl_scales[q][:],
                     start=(q == 0),
                     stop=(q == PASSES - 1),
                 )
-            live["al", c, t] = bank
-
-        def activate(c, t):
-            bank = live["al", c, t]
             nc.scalar.activation(out=th[c][:, t, :], in_=bank[:, 0, :], func=ACT.Tanh, bias=bias[:, c, t : t + 1])
-            nc.scalar.activation(out=la_gain[c][:, t, :], in_=bank[:, 1, :], func=ACT.Copy, scale=neg_gain[:, c, t : t + 1])
-
-        def apply_gain(c, t):
-            nc.vector.tensor_scalar(
-                out=th_gain[c][:, t, :], in0=th[c][:, t, :], scalar1=gain[:, c, t : t + 1], scalar2=None, op0=ALU.mult
+            nc.scalar.activation(
+                out=la_gain[c][:, t, :], in_=bank[:, 1, :], func=ACT.Copy, scale=neg_gain[:, c, t : t + 1]
             )
+
+        def apply_gain(c):
+            for t in range(SLOTS):
+                nc.vector.tensor_scalar(
+                    out=th_gain[c][:, t, :], in0=th[c][:, t, :], scalar1=gain[:, c, t : t + 1], scalar2=None, op0=ALU.mult
+                )
 
         def square_th(h, c):
             nc.scalar.activation(
-                out=th_sq[h][c][:], in_=th[c][:, :, h * P : (h + 1) * P].rearrange("p t n -> p n t"), func=ACT.Square
+                out=th_sq[h][c][:], in_=th[c][:, :, tokens(h)].rearrange("p t n -> p n t"), func=ACT.Square
             )
 
         def round_y(c):
-            y_in = work.tile([P, N, PACK], BF16, name="y_in", bufs=2, align_bytes=64)
+            y_in = work.tile([P, N, SLOTS], BF16, name="y_in", align_bytes=64)
             nc.vector.tensor_copy(out=y_in[:], in_=th_gain[c][:].rearrange("p t n -> p n t"))
             live["y_in", c] = y_in
 
         def quantize_y(c):
             nc.vector.quantize_mx(
-                out=y_codes[c][:].bitcast(FP8X4), scales=y_scales[c][:], in_=live["y_in", c][:].rearrange("p n t -> p (n t)")
+                out=y_codes[c][:].bitcast(FP8X4),
+                scales=y_scales[c][:],
+                in_=live["y_in", c][:].rearrange("p n t -> p (n t)"),
             )
 
         def lap_product(h, c):
-            u = work.tile([P, PACK, P], F32, name="lap_u", bufs=2)
+            curve = work.tile([P, SLOTS, P], F32, name="curve")
             nc.vector.scalar_tensor_tensor(
-                out=u[:], in0=live["sum", h, c][:], scalar=2.0, in1=th_gain[c][:, :, h * P : (h + 1) * P],
-                op0=ALU.mult, op1=ALU.mult,
+                out=curve[:],
+                in0=live["sum", h, c][:],
+                scalar=2.0,
+                in1=th_gain[c][:, :, tokens(h)],
+                op0=ALU.mult,
+                op1=ALU.mult,
             )
-            live["u", h, c] = u
+            live["curve", h, c] = curve
 
         def lap_sum(h, c):
-            v = work.tile([P, PACK, P], F32, name="lap_v", bufs=2)
-            nc.vector.tensor_tensor(out=v[:], in0=live["u", h, c][:], in1=la_gain[c][:, :, h * P : (h + 1) * P], op=ALU.add)
-            live["v", h, c] = v
+            inner = work.tile([P, SLOTS, P], F32, name="inner")
+            nc.vector.tensor_tensor(
+                out=inner[:], in0=live["curve", h, c][:], in1=la_gain[c][:, :, tokens(h)], op=ALU.add
+            )
+            live["inner", h, c] = inner
+
+        def times_th_sq_less_one(dst, h, c, src):
+            nc.vector.scalar_tensor_tensor(
+                out=dst,
+                in0=th_sq[h][c][:],
+                scalar=-1.0,
+                in1=src.rearrange("p t n -> p n t"),
+                op0=ALU.add,
+                op1=ALU.mult,
+            )
 
         def lap_round(h, c):
-            lap_in = work.tile([P, P, PACK], BF16, name="lap_in", bufs=2, align_bytes=64)
-            nc.vector.scalar_tensor_tensor(
-                out=lap_in[:], in0=th_sq[h][c][:], scalar=-1.0, in1=live["v", h, c][:].rearrange("p t n -> p n t"),
-                op0=ALU.add, op1=ALU.mult,
-            )
+            lap_in = work.tile([P, P, SLOTS], BF16, name="lap_in", align_bytes=64)
+            times_th_sq_less_one(lap_in[:], h, c, live["inner", h, c][:])
+            live["lap_in", h, c] = lap_in
+
+        def lap_factors(h, c):
+            for name, src in (("slope", th_gain), ("base", la_gain)):
+                live[name] = work.tile([P, P, SLOTS], F32, name=name, bufs=1)
+                times_th_sq_less_one(live[name][:], h, c, src[c][:, :, tokens(h)])
+
+        def lap_from_factors(h, c):
+            term = work.tile([P, P, SLOTS], F32, name="term", bufs=1)
+            lap_in = work.tile([P, P, SLOTS], BF16, name="lap_in", align_bytes=64)
+            ranges = [slice(0, P // 2), slice(P // 2, P)]
+            for part in ranges:
+                nc.vector.scalar_tensor_tensor(
+                    out=term[:, part, :],
+                    in0=live["sum", h, c][:, :, part].rearrange("p t n -> p n t"),
+                    scalar=2.0,
+                    in1=live["slope"][:, part, :],
+                    op0=ALU.mult,
+                    op1=ALU.mult,
+                )
+            for part in ranges:
+                nc.vector.tensor_tensor(
+                    out=lap_in[:, part, :], in0=term[:, part, :], in1=live["base"][:, part, :], op=ALU.add
+                )
             live["lap_in", h, c] = lap_in
 
         def quantize_lap(h, c):
@@ -251,218 +300,169 @@ def tile_forwardlaplaciantanhlayer_w4_kernel(
                 in_=live["lap_in", h, c][:].rearrange("p n t -> p (n t)"),
             )
 
-        def lap_factors(h, c):
-            tokens = slice(h * P, (h + 1) * P)
-            for name, src in (("slope", th_gain), ("base", la_gain)):
-                dst = work.tile([P, P, PACK], F32, name=name, bufs=1)
-                nc.vector.scalar_tensor_tensor(
-                    out=dst[:], in0=th_sq[h][c][:], scalar=-1.0, in1=src[c][:, :, tokens].rearrange("p t n -> p n t"),
-                    op0=ALU.add, op1=ALU.mult,
-                )
-                live[name] = dst
+        def product_out(dst, h, codes, scales, last=False):
+            banks = [psum.tile([P, BANK], F32, name="product", bufs=PRODUCT_BANKS) for n in range(COLS)]
+            for c in range(GROUPS):
+                for n in range(COLS):
+                    nc.tensor.matmul_mx(
+                        out=banks[n][:],
+                        lhsT=codes[c].bitcast(FP8X4),
+                        lhsT_scale=scales[c],
+                        rhs=w2[:, c, W4 * BANK * n : W4 * BANK * (n + 1)].bitcast(FP4X4),
+                        rhs_scale=s2[:, c, BANK * n : BANK * (n + 1)],
+                        start=(c == 0),
+                        stop=(c == GROUPS - 1),
+                    )
+            for n in range(COLS):
+                result = work.tile([P, BANK], F32, name="result", bufs=2 * HALVES * COLS)
+                if last and n == 0:
+                    nc.vector.tensor_copy(out=result[:], in_=banks[n][:])
+                else:
+                    nc.scalar.copy(out=result[:], in_=banks[n][:])
+                nc.sync.dma_start(out=dst[tokens(h), n * BANK : (n + 1) * BANK], in_=result[:])
 
-        def lap_last(h, c):
-            term = work.tile([P, P, PACK], F32, name="term", bufs=1)
-            lap_in = work.tile([P, P, PACK], BF16, name="lap_in", bufs=2, align_bytes=64)
-            halves = [slice(0, P // 2), slice(P // 2, P)]
-            for part in halves:
-                nc.vector.scalar_tensor_tensor(
-                    out=term[:, part, :], in0=live["sum", h, c][:, :, part].rearrange("p t n -> p n t"), scalar=2.0,
-                    in1=live["slope"][:, part, :], op0=ALU.mult, op1=ALU.mult,
-                )
-            for part in halves:
-                nc.vector.tensor_tensor(out=lap_in[:, part, :], in0=term[:, part, :], in1=live["base"][:, part, :], op=ALU.add)
-            live["lap_in", h, c] = lap_in
+        def product_y(h):
+            product_out(out_1, h, [a[:, tokens(h)] for a in y_codes], [a[:, tokens(h)] for a in y_scales])
 
-        def multiply_out(key, codes, scales, c):
-            for n in range(2):
-                if c == 0:
-                    live[key, n] = psum.tile([P, BANK], F32, name="acc", bufs=4)
-                nc.tensor.matmul_mx(
-                    out=live[key, n][:],
-                    lhsT=codes.bitcast(FP8X4),
-                    lhsT_scale=scales,
-                    rhs=w2[:, c, 2 * BANK * n : 2 * BANK * (n + 1)].bitcast(FP4X4),
-                    rhs_scale=s2[:, c, BANK * n : BANK * (n + 1)],
-                    start=(c == 0),
-                    stop=(c == 1),
-                )
+        def product_lap(h):
+            product_out(out_0, h, [a[:] for a in lap_codes[h]], [a[:] for a in lap_scales[h]], last=(h == HALVES - 1))
 
-        def multiply_y(h, c):
-            multiply_out(("y", h), y_codes[c][:, h * P : (h + 1) * P], y_scales[c][:, h * P : (h + 1) * P], c)
-
-        def multiply_lap(h, c):
-            multiply_out(("lap", h), lap_codes[h][c][:], lap_scales[h][c][:], c)
-
-        def store(key, dst, h, n, on_vector):
-            result = work.tile([P, BANK], F32, name="result", bufs=8)
-            if on_vector:
-                nc.vector.tensor_copy(out=result[:], in_=live[(key, h), n][:])
-            else:
-                nc.scalar.copy(out=result[:], in_=live[(key, h), n][:])
-            nc.sync.dma_start(out=dst[h * P : (h + 1) * P, n * BANK : (n + 1) * BANK], in_=result[:])
-
-        nc.sync.dma_start(out=scale_col[:], in_=j_scale.rearrange("a o (q p t) -> p (a o q) t", p=P, t=PACK))
         nc.vector.memset(s1[:].bitcast(I32), 0)
-        nc.vector.memset(warm[:], 0.0)
+        nc.vector.memset(table_in[:], 0.0)
         nc.vector.memset(s2[:].bitcast(I32), 0)
         make_identity(nc, ident[:])
-        nc.scalar.activation(out=warm_out[:], in_=warm[:], func=ACT.Tanh)
-        load_j(0)
+        nc.scalar.activation(out=table_out[:], in_=table_in[:], func=ACT.Tanh)
+
+        by_slot = "(c p t) -> p c t"
+        nc.sync.dma_start(out=scale_col[:], in_=j_scale.rearrange("a o (q p t) -> p (a o q) t", p=P, t=SLOTS))
+        load_words(w1[0], w1_words[:, :, : W4 * PASS])
         load_scales(s1, w1_scales)
-        load_words(w1[0], w1_words[:, :, : 2 * PASS])
-        nc.sync.dma_start(out=rows_bf[0][:], in_=x.rearrange("(h p) d -> p h d", p=P))
+        load_j(0)
+        nc.sync.dma_start(out=xl_rows[0][:], in_=x.rearrange("(h p) d -> p h d", p=P))
         load_j(1)
-        nc.sync.dma_start(out=rows_bf[1][:], in_=l.rearrange("(h p) d -> p h d", p=P))
-        load_words(w1[1], w1_words[:, :, 2 * PASS :])
+        nc.sync.dma_start(out=xl_rows[1][:], in_=l.rearrange("(h p) d -> p h d", p=P))
         load_j(2)
-        nc.sync.dma_start(out=b_raw[:], in_=b.rearrange("(q p t) -> p q t", p=P, t=PACK))
-        nc.sync.dma_start(out=g_raw[:], in_=g.rearrange("(q p t) -> p q t", p=P, t=PACK))
+        nc.sync.dma_start(out=bias[:], in_=b.rearrange(by_slot, p=P, t=SLOTS))
+        nc.sync.dma_start(out=gain[:], in_=g.rearrange(by_slot, p=P, t=SLOTS))
+        load_words(w1[1], w1_words[:, :, W4 * PASS :])
         for s in range(3, J_TILES):
             load_j(s)
         load_scales(s2, w2_scales)
         load_words(w2, w2_words)
 
-        def al(i):
-            c, t = divmod(i, PACK)
-            multiply_xl(c, t)
-            activate(c, t)
-
-        def jm(s, c):
-            multiply_j(s, c)
-            square(s, c)
-
-        def gains(c):
-            for t in range(PACK):
-                apply_gain(c, t)
-
-        def turn(s):
-            turn_j(s)
-            empty_j(s)
-
         for q in range(PASSES):
             spread_scale(q)
+        for q in range(PASSES):
+            order_words(0, q)
+        widen(0, parts=PASSES)
         order_scales(0)
-        widen(0, 2)
-        order_words(0, 0)
-        turn(0)
         widen(1)
         turn_xl(0, 0)
-        empty_xl(0, 0)
-        quantize_j(0)
+        turn_j(0)
         turn_xl(0, 1)
-        empty_xl(0, 1)
-        jm(0, 0)
-        turn(1)
-        widen(2)
+        quantize_j(0)
         turn_xl(1, 0)
-        empty_xl(1, 0)
-        jm(0, 1)
-        quantize_j(1)
-        order_words(0, 1)
+        widen(2)
+        product_j(0, 0)
         turn_xl(1, 1)
-        empty_xl(1, 1)
-        turn(2)
-        nc.vector.tensor_copy(out=bias[:], in_=b_raw[:])
-        nc.vector.tensor_copy(out=gain[:], in_=g_raw[:])
-        nc.vector.tensor_scalar(out=neg_gain[:], in0=g_raw[:], scalar1=-1.0, scalar2=None, op0=ALU.mult)
+        turn_j(1)
         quantize_xl(0)
-        widen(3)
-        jm(1, 0)
-        jm(1, 1)
+        nc.vector.tensor_scalar(out=neg_gain[:], in0=gain[:], scalar1=-1.0, scalar2=None, op0=ALU.mult)
         quantize_xl(1)
+        quantize_j(1)
+        product_j(0, 1)
+
+
+        turn_j(2)
+        widen(3)
+        product_xl(0, 0)
+        product_xl(0, 1)
+        product_j(1, 0)
+        product_j(1, 1)
         quantize_j(2)
-        turn(3)
-        fold(0, 0)
-        fold(0, 1)
-        widen(4)
         order_scales(1)
-        quantize_j(3)
-        al(0)
-        jm(2, 0)
-        al(1)
-        jm(2, 1)
-        turn(4)
-        fold(1, 0)
-        fold(1, 1)
-        widen(5)
         order_words(1, 0)
-        quantize_j(4)
+
+        turn_j(3)
+        fold(0, 1, opens=True)
+        add_pair(1, 0)
+        widen(4)
+        product_xl(0, 2)
+        product_xl(0, 3)
+        product_j(2, 0)
+        product_j(2, 1)
+        quantize_j(3)
         order_words(1, 1)
-        al(2)
-        jm(3, 0)
-        al(3)
-        jm(3, 1)
-        turn(5)
-        fold(2, 0)
-        fold(2, 1)
-        widen(6)
-        gains(0)
-        quantize_j(5)
-        al(4)
-        jm(4, 0)
-        al(5)
-        round_y(0)
-        turn(6)
-        fold(3, 0)
-        fold(3, 1)
-        widen(7)
-        quantize_j(6)
-        lap_product(0, 0)
-        quantize_y(0)
-        al(6)
-        jm(5, 0)
-        al(7)
+
+        turn_j(4)
+        fold(1, 0, opens=True)
+        fold(1, 1)
         square_th(0, 0)
+        widen(5)
+        apply_gain(0)
+        quantize_j(4)
+        widen(6)
+        product_xl(1, 0)
+        product_j(3, 0)
+        product_xl(1, 1)
+        product_j(3, 1)
+        round_y(0)
+
+        turn_j(5)
+        fold(2, 0)
+        fold(3, 0)
+        quantize_y(0)
+        widen(7)
+        lap_product(0, 0)
+        quantize_j(5)
+        add_pair(3, 1)
+        product_xl(1, 2)
+        product_xl(1, 3)
+        product_j(4, 0)
+        product_j(5, 0)
         lap_sum(0, 0)
-        turn(7)
-        fold(4, 0)
-        fold(5, 0)
-        gains(1)
-        quantize_j(7)
-        lap_product(0, 1)
-        jm(6, 0)
-        jm(4, 1)
+
+        turn_j(6)
+        turn_j(7)
+        fold(3, 1)
         square_th(0, 1)
-        round_y(1)
+        apply_gain(1)
         lap_round(0, 0)
-        lap_sum(0, 1)
+        lap_product(0, 1)
+        quantize_j(6)
+        round_y(1)
+        quantize_j(7)
+        add_pair(5, 0)
+        product_j(4, 1)
+        product_j(5, 1)
+        product_j(6, 0)
+        product_j(7, 0)
+        square_th(1, 1)
         quantize_y(1)
-        jm(7, 0)
-        jm(5, 1)
-        square_th(1, 0)
-        fold(6, 0)
-        fold(4, 1)
-        fold(7, 0)
+        lap_sum(0, 1)
         quantize_lap(0, 0)
+
+        fold(5, 0, opens=True)
+        fold(6, 0)
+        fold(7, 0)
         lap_round(0, 1)
+        add_pair(5, 1)
         lap_product(1, 0)
         quantize_lap(0, 1)
-        jm(6, 1)
-        square_th(1, 1)
-        jm(7, 1)
+        product_j(6, 1)
+        product_j(7, 1)
+        square_th(1, 0)
+        product_y(0)
         lap_sum(1, 0)
-        multiply_y(0, 0)
-        multiply_y(0, 1)
         lap_factors(1, 1)
-        fold(5, 1)
+
+        fold(5, 1, opens=True)
         fold(6, 1)
         fold(7, 1)
         lap_round(1, 0)
-        for n in range(2):
-            store("y", out_1, 0, n, False)
-        multiply_y(1, 0)
-        multiply_y(1, 1)
-        lap_last(1, 1)
-        quantize_lap(1, 0)
-        quantize_lap(1, 1)
-        for n in range(2):
-            store("y", out_1, 1, n, False)
-        multiply_lap(0, 0)
-        multiply_lap(0, 1)
-        for n in range(2):
-            store("lap", out_0, 0, n, n == 0)
-        multiply_lap(1, 0)
-        multiply_lap(1, 1)
-        for n in range(2):
-            store("lap", out_0, 1, n, n == 0)
+        lap_from_factors(1, 1)
+        for c in range(GROUPS):
+            quantize_lap(1, c)
+        product_y(1)
+        product_lap(0)
+        product_lap(1)

@@ -49,8 +49,7 @@ def tile_forwardlaplaciantanhlayer_w4_kernel(
             return [kept("%s%d" % (name, c), shape, dtype) for c in range(GROUPS)]
 
         ident = kept("ident", [P, P], F32)
-        table_in = kept("table_in", [P, 8], F32)
-        table_out = kept("table_out", [P, 8], F32)
+        idle = kept("idle", [P, BANK], BF16)
         scale_col = kept("scale_col", [P, PASSES, SLOTS], F32)
         scale_row = kept("scale_row", [P, D], F32)
         bias = kept("bias", [P, GROUPS, SLOTS], BF16)
@@ -101,10 +100,16 @@ def tile_forwardlaplaciantanhlayer_w4_kernel(
             bank = psum.tile([P, SLOTS, P], F32, name="sum%d" % q)
             for t in range(SLOTS):
                 nc.tensor.transpose(bank[:, t, :], scale_col[:, q, t : t + 1].to_broadcast([P, P]), ident[:])
-            nc.scalar.copy(
+            nc.scalar.activation(
                 out=scale_row[:, q * PASS : (q + 1) * PASS].rearrange("p (n t) -> p n t", t=SLOTS),
                 in_=bank[:].rearrange("p t n -> p n t"),
+                func=ACT.Copy,
             )
+
+        def warm_up(count):
+            bank = psum.tile([P, BANK], F32, name="product", bufs=PRODUCT_BANKS)
+            for step in range(count):
+                nc.tensor.matmul(bank[:], lhsT=idle[:, :P], rhs=idle[:], start=True, stop=True)
 
         def every_second_word(q, u):
             return slice(PASS_WORDS * q + u, PASS_WORDS * (q + 1), 2)
@@ -327,11 +332,10 @@ def tile_forwardlaplaciantanhlayer_w4_kernel(
         def product_lap(h):
             product_out(out_0, h, [a[:] for a in lap_codes[h]], [a[:] for a in lap_scales[h]], last=(h == HALVES - 1))
 
+        nc.vector.memset(idle[:], 0.0)
         nc.vector.memset(s1[:].bitcast(I32), 0)
-        nc.vector.memset(table_in[:], 0.0)
         nc.vector.memset(s2[:].bitcast(I32), 0)
         make_identity(nc, ident[:])
-        nc.scalar.activation(out=table_out[:], in_=table_in[:], func=ACT.Tanh)
 
         by_slot = "(c p t) -> p c t"
         nc.sync.dma_start(out=scale_col[:], in_=j_scale.rearrange("a o (q p t) -> p (a o q) t", p=P, t=SLOTS))
@@ -350,8 +354,10 @@ def tile_forwardlaplaciantanhlayer_w4_kernel(
         load_scales(s2, w2_scales)
         load_words(w2, w2_words)
 
+        warm_up(3)
         for q in range(PASSES):
             spread_scale(q)
+        warm_up(4)
         for q in range(PASSES):
             order_words(0, q)
         widen(0, parts=PASSES)
@@ -359,6 +365,7 @@ def tile_forwardlaplaciantanhlayer_w4_kernel(
         widen(1)
         turn_xl(0, 0)
         turn_j(0)
+        warm_up(2)
         turn_xl(0, 1)
         quantize_j(0)
         turn_xl(1, 0)

@@ -115,7 +115,7 @@ def tile_forwardlaplaciantanhlayer_w4_kernel(
             return slice(PASS_WORDS * q + u, PASS_WORDS * (q + 1), 2)
 
         def turn_xl(i, q):
-            bank = psum.tile([P, 2, N], F32, name="turn", bufs=TURN_BANKS)
+            bank = psum.tile([P, 2, N], F32, name="product", bufs=PRODUCT_BANKS)
             words = xl_rows[i][:].bitcast(F32)
             for h in range(HALVES):
                 for u in range(2):
@@ -180,7 +180,7 @@ def tile_forwardlaplaciantanhlayer_w4_kernel(
             live["squares", s, c] = squares
 
         def add_pair(s, c):
-            pair = work.tile([P, SLOTS, P], F32, name="pair")
+            pair = work.tile([P, SLOTS, P], F32, name="pair", bufs=3)
             nc.vector.tensor_tensor(
                 out=pair[:], in0=live["squares", s - 1, c][:], in1=live["squares", s, c][:], op=ALU.add
             )
@@ -240,63 +240,45 @@ def tile_forwardlaplaciantanhlayer_w4_kernel(
                 in_=live["y_in", c][:].rearrange("p n t -> p (n t)"),
             )
 
-        def lap_product(h, c):
-            curve = work.tile([P, SLOTS, P], F32, name="curve")
+        def lap_product(h, c, part=slice(0, P)):
+            curve = work.tile([P, SLOTS, part.stop - part.start], F32, name="curve")
+            live["curve", h, c, part.start] = curve
             nc.vector.scalar_tensor_tensor(
                 out=curve[:],
-                in0=live["sum", h, c][:],
+                in0=live["sum", h, c][:, :, part],
                 scalar=2.0,
-                in1=th_gain[c][:, :, tokens(h)],
+                in1=th_gain[c][:, :, tokens(h)][:, :, part],
                 op0=ALU.mult,
                 op1=ALU.mult,
             )
-            live["curve", h, c] = curve
 
-        def lap_sum(h, c):
-            inner = work.tile([P, SLOTS, P], F32, name="inner")
+        def lap_sum(h, c, part=slice(0, P)):
+            inner = work.tile([P, SLOTS, part.stop - part.start], F32, name="inner")
+            live["inner", h, c, part.start] = inner
             nc.vector.tensor_tensor(
-                out=inner[:], in0=live["curve", h, c][:], in1=la_gain[c][:, :, tokens(h)], op=ALU.add
+                out=inner[:],
+                in0=live["curve", h, c, part.start][:],
+                in1=la_gain[c][:, :, tokens(h)][:, :, part],
+                op=ALU.add,
             )
-            live["inner", h, c] = inner
 
-        def times_th_sq_less_one(dst, h, c, src):
+        def lap_round(h, c, part=slice(0, P)):
+            if part.start == 0:
+                live["lap_in", h, c] = work.tile([P, P, SLOTS], BF16, name="lap_in", align_bytes=64)
             nc.vector.scalar_tensor_tensor(
-                out=dst,
-                in0=th_sq[h][c][:],
+                out=live["lap_in", h, c][:, part, :],
+                in0=th_sq[h][c][:, part, :],
                 scalar=-1.0,
-                in1=src.rearrange("p t n -> p n t"),
+                in1=live["inner", h, c, part.start][:].rearrange("p t n -> p n t"),
                 op0=ALU.add,
                 op1=ALU.mult,
             )
 
-        def lap_round(h, c):
-            lap_in = work.tile([P, P, SLOTS], BF16, name="lap_in", align_bytes=64)
-            times_th_sq_less_one(lap_in[:], h, c, live["inner", h, c][:])
-            live["lap_in", h, c] = lap_in
-
-        def lap_factors(h, c):
-            for name, src in (("slope", th_gain), ("base", la_gain)):
-                live[name] = work.tile([P, P, SLOTS], F32, name=name, bufs=1)
-                times_th_sq_less_one(live[name][:], h, c, src[c][:, :, tokens(h)])
-
-        def lap_from_factors(h, c):
-            term = work.tile([P, P, SLOTS], F32, name="term", bufs=1)
-            lap_in = work.tile([P, P, SLOTS], BF16, name="lap_in", align_bytes=64)
+        def lap_last(h, c):
             ranges = [slice(0, P // 2), slice(P // 2, P)]
-            for part in ranges:
-                nc.vector.scalar_tensor_tensor(
-                    out=term[:, part, :],
-                    in0=live["sum", h, c][:, :, part].rearrange("p t n -> p n t"),
-                    scalar=2.0,
-                    in1=live["slope"][:, part, :],
-                    op0=ALU.mult,
-                    op1=ALU.mult,
-                )
-            for part in ranges:
-                nc.vector.tensor_tensor(
-                    out=lap_in[:, part, :], in0=term[:, part, :], in1=live["base"][:, part, :], op=ALU.add
-                )
-            live["lap_in", h, c] = lap_in
+            for step in (lap_product, lap_sum, lap_round):
+                for part in ranges:
+                    step(h, c, part)
 
         def quantize_lap(h, c):
             nc.vector.quantize_mx(
@@ -307,8 +289,8 @@ def tile_forwardlaplaciantanhlayer_w4_kernel(
 
         def product_out(dst, h, codes, scales, last=False):
             banks = [psum.tile([P, BANK], F32, name="product", bufs=PRODUCT_BANKS) for n in range(COLS)]
-            for c in range(GROUPS):
-                for n in range(COLS):
+            for n in range(COLS):
+                for c in range(GROUPS):
                     nc.tensor.matmul_mx(
                         out=banks[n][:],
                         lhsT=codes[c].bitcast(FP8X4),
@@ -332,17 +314,17 @@ def tile_forwardlaplaciantanhlayer_w4_kernel(
         def product_lap(h):
             product_out(out_0, h, [a[:] for a in lap_codes[h]], [a[:] for a in lap_scales[h]], last=(h == HALVES - 1))
 
-        nc.vector.memset(idle[:], 0.0)
         nc.vector.memset(s1[:].bitcast(I32), 0)
         nc.vector.memset(s2[:].bitcast(I32), 0)
+        nc.gpsimd.memset(idle[:], 0.0)
         make_identity(nc, ident[:])
 
         by_slot = "(c p t) -> p c t"
         nc.sync.dma_start(out=scale_col[:], in_=j_scale.rearrange("a o (q p t) -> p (a o q) t", p=P, t=SLOTS))
         load_words(w1[0], w1_words[:, :, : W4 * PASS])
-        load_scales(s1, w1_scales)
         load_j(0)
         nc.sync.dma_start(out=xl_rows[0][:], in_=x.rearrange("(h p) d -> p h d", p=P))
+        load_scales(s1, w1_scales)
         load_j(1)
         nc.sync.dma_start(out=xl_rows[1][:], in_=l.rearrange("(h p) d -> p h d", p=P))
         load_j(2)
@@ -363,47 +345,46 @@ def tile_forwardlaplaciantanhlayer_w4_kernel(
         widen(0, parts=PASSES)
         order_scales(0)
         widen(1)
-        turn_xl(0, 0)
+        for q in range(PASSES):
+            turn_xl(0, q)
         turn_j(0)
         warm_up(2)
-        turn_xl(0, 1)
         quantize_j(0)
-        turn_xl(1, 0)
         widen(2)
-        product_j(0, 0)
-        turn_xl(1, 1)
-        turn_j(1)
-        quantize_xl(0)
+        for q in range(PASSES):
+            turn_xl(1, q)
+            quantize_xl(q)
         nc.vector.tensor_scalar(out=neg_gain[:], in0=gain[:], scalar1=-1.0, scalar2=None, op0=ALU.mult)
-        quantize_xl(1)
-        quantize_j(1)
-        product_j(0, 1)
+        for c in range(GROUPS):
+            product_j(0, c)
 
 
+        turn_j(1)
         turn_j(2)
         widen(3)
+        quantize_j(1)
+        order_scales(1)
         product_xl(0, 0)
         product_xl(0, 1)
         product_j(1, 0)
         product_j(1, 1)
         quantize_j(2)
-        order_scales(1)
         order_words(1, 0)
+        order_words(1, 1)
 
         turn_j(3)
-        fold(0, 1, opens=True)
         add_pair(1, 0)
         widen(4)
+        add_pair(1, 1)
         product_xl(0, 2)
         product_xl(0, 3)
         product_j(2, 0)
         product_j(2, 1)
         quantize_j(3)
-        order_words(1, 1)
 
         turn_j(4)
         fold(1, 0, opens=True)
-        fold(1, 1)
+        fold(2, 0)
         square_th(0, 0)
         widen(5)
         apply_gain(0)
@@ -414,37 +395,37 @@ def tile_forwardlaplaciantanhlayer_w4_kernel(
         product_xl(1, 1)
         product_j(3, 1)
         round_y(0)
+        widen(7)
 
         turn_j(5)
-        fold(2, 0)
+        turn_j(6)
         fold(3, 0)
         quantize_y(0)
-        widen(7)
         lap_product(0, 0)
         quantize_j(5)
         add_pair(3, 1)
+        quantize_j(6)
         product_xl(1, 2)
         product_xl(1, 3)
         product_j(4, 0)
         product_j(5, 0)
         lap_sum(0, 0)
 
-        turn_j(6)
         turn_j(7)
+        fold(1, 1, opens=True)
         fold(3, 1)
         square_th(0, 1)
         apply_gain(1)
         lap_round(0, 0)
         lap_product(0, 1)
-        quantize_j(6)
-        round_y(1)
         quantize_j(7)
+        round_y(1)
         add_pair(5, 0)
-        product_j(4, 1)
-        product_j(5, 1)
         product_j(6, 0)
+        product_j(4, 1)
         product_j(7, 0)
-        square_th(1, 1)
+        product_j(5, 1)
+        square_th(1, 0)
         quantize_y(1)
         lap_sum(0, 1)
         quantize_lap(0, 0)
@@ -458,18 +439,17 @@ def tile_forwardlaplaciantanhlayer_w4_kernel(
         quantize_lap(0, 1)
         product_j(6, 1)
         product_j(7, 1)
-        square_th(1, 0)
+        square_th(1, 1)
         product_y(0)
         lap_sum(1, 0)
-        lap_factors(1, 1)
+        lap_round(1, 0)
 
         fold(5, 1, opens=True)
         fold(6, 1)
         fold(7, 1)
-        lap_round(1, 0)
-        lap_from_factors(1, 1)
-        for c in range(GROUPS):
-            quantize_lap(1, c)
+        quantize_lap(1, 0)
+        lap_last(1, 1)
+        quantize_lap(1, 1)
         product_y(1)
         product_lap(0)
         product_lap(1)

@@ -225,12 +225,16 @@ def tile_forwardlaplaciantanhlayer_w4_kernel(
 
         def square_th(h, c):
             nc.scalar.activation(
-                out=th_sq[h][c][:], in_=th[c][:, :, tokens(h)].rearrange("p t n -> p n t"), func=ACT.Square
+                out=th_sq[h][c][:].rearrange("p (a i) t -> p a t i", i=4),
+                in_=th[c][:, :, tokens(h)].rearrange("p t (a i) -> p a t i", i=4),
+                func=ACT.Square,
             )
 
         def round_y(c):
             y_in = work.tile([P, N, SLOTS], BF16, name="y_in", align_bytes=64)
-            nc.vector.tensor_copy(out=y_in[:], in_=th_gain[c][:].rearrange("p t n -> p n t"))
+            nc.vector.tensor_copy(
+                out=y_in[:].rearrange("p (a i) t -> p a t i", i=4), in_=th_gain[c][:].rearrange("p t (a i) -> p a t i", i=4)
+            )
             live["y_in", c] = y_in
 
         def quantize_y(c):

from contextlib import ExitStack

import concourse.mybir as mybir
from concourse.masks import make_identity

N, K, D, F, P_OUT = 256, 4, 1024, 1024, 1024
FLOPS = 2 * (K + 2) * N * D * F + 2 * 2 * N * F * P_OUT

F32 = mybir.dt.float32
BF16 = mybir.dt.bfloat16
I32 = mybir.dt.int32
U32 = mybir.dt.uint32
U8 = mybir.dt.uint8
FP8 = mybir.dt.float8_e4m3fn
FP8X4 = mybir.dt.float8_e4m3fn_x4
FP4X4 = mybir.dt.float4_e2m1fn_x4
ALU = mybir.AluOpType
ACT = mybir.ActivationFunctionType

P = 128
SLOTS = 4
PASS = P * SLOTS
PASSES = D // PASS
GROUPS = F // PASS
HALVES = N // P
BANK = 512
COLS = P_OUT // BANK
J_TILES = HALVES * K
PASS_WORDS = PASS // 2
W4 = 2
LINE = 16
TURN_BANKS, PRODUCT_BANKS = 2, 4


def tile_forwardlaplaciantanhlayer_w4_kernel(
    tc, x, j_bytes, j_scale, l, w1_words, w1_scales, b, g, w2_words, w2_scales, out_0, out_1
):
    nc = tc.nc
    with ExitStack() as ctx:
        keep = ctx.enter_context(tc.tile_pool(name="keep", bufs=1))
        work = ctx.enter_context(tc.tile_pool(name="work", bufs=2))
        psum = ctx.enter_context(tc.psum_pool(name="psum", bufs=1))
        ctx.enter_context(tc.manual_schedule())

        def kept(name, shape, dtype):
            return keep.tile(shape, dtype, name=name, align_bytes=64)

        def per_group(name, shape, dtype):
            return [kept("%s%d" % (name, c), shape, dtype) for c in range(GROUPS)]

        ident = kept("ident", [P, P], F32)
        idle = kept("idle", [P, BANK], BF16)
        scale_col = kept("scale_col", [P, PASSES, SLOTS], F32)
        scale_row = kept("scale_row", [P, D], F32)
        bias = kept("bias", [P, GROUPS, SLOTS], BF16)
        gain = kept("gain", [P, GROUPS, SLOTS], BF16)
        neg_gain = kept("neg_gain", [P, GROUPS, SLOTS], F32)
        w1 = per_group("w1_", [P, PASSES, W4 * PASS], U8)
        s1 = kept("s1", [P, PASSES, F], U8)
        w2 = kept("w2", [P, GROUPS, W4 * P_OUT], U8)
        s2 = kept("s2", [P, GROUPS, P_OUT], U8)
        w1_by_slot = per_group("w1_by_slot", [P, PASSES, W4 * PASS], U8)
        s1_by_slot = per_group("s1_by_slot", [P, PASSES, PASS], U8)
        xl_rows = [kept("xl_rows%d" % i, [P, HALVES, D], BF16) for i in range(2)]
        j_rows = [kept("j_rows%d" % s, [P, D], U8) for s in range(J_TILES)]
        xl_turned = [kept("xl_turned%d" % q, [P, 2 * N * SLOTS], BF16) for q in range(PASSES)]
        xl_codes = [kept("xl_codes%d" % q, [P, 2 * N], U32) for q in range(PASSES)]
        xl_scales = [kept("xl_scales%d" % q, [P, 2 * N], U8) for q in range(PASSES)]
        j_codes = [kept("j_codes%d" % s, [P, PASSES * P], U32) for s in range(J_TILES)]
        j_scales = [kept("j_scales%d" % s, [P, PASSES * P], U8) for s in range(J_TILES)]
        th = per_group("th", [P, SLOTS, N], F32)
        th_gain = per_group("th_gain", [P, SLOTS, N], F32)
        la_gain = per_group("la_gain", [P, SLOTS, N], F32)
        th_sq = [per_group("th_sq%d_" % h, [P, P, SLOTS], F32) for h in range(HALVES)]
        y_codes = per_group("y_codes", [P, N], U32)
        y_scales = per_group("y_scales", [P, N], U8)
        lap_codes = [per_group("lap_codes%d_" % h, [P, P], U32) for h in range(HALVES)]
        lap_scales = [per_group("lap_scales%d_" % h, [P, P], U8) for h in range(HALVES)]

        live = {}

        def tokens(h):
            return slice(h * P, (h + 1) * P)

        def load_words(dst, src):
            nc.sync.dma_start(out=dst[:].bitcast(I32), in_=src.rearrange("q p n -> p q n").bitcast(I32))

        def load_scales(dst, src):
            for quad in range(4):
                nc.sync.dma_start(
                    out=dst[32 * quad : 32 * quad + 4].bitcast(I32),
                    in_=src[:, 4 * quad : 4 * quad + 4, :].rearrange("q r n -> r q n").bitcast(I32),
                )

        def load_j(s):
            h, k = divmod(s, K)
            nc.sync.dma_start(out=j_rows[s][:], in_=j_bytes[k, tokens(h), :])

        def spread_scale(q):
            bank = psum.tile([P, SLOTS, P], F32, name="sum%d" % q)
            for t in range(SLOTS):
                nc.tensor.transpose(bank[:, t, :], scale_col[:, q, t : t + 1].to_broadcast([P, P]), ident[:])
            nc.scalar.activation(
                out=scale_row[:, q * PASS : (q + 1) * PASS].rearrange("p (n t) -> p n t", t=SLOTS),
                in_=bank[:].rearrange("p t n -> p n t"),
                func=ACT.Copy,
            )

        def warm_up(count):
            bank = psum.tile([P, BANK], F32, name="product", bufs=PRODUCT_BANKS)
            for step in range(count):
                nc.tensor.matmul(bank[:], lhsT=idle[:, :P], rhs=idle[:], start=True, stop=True)

        def every_second_word(q, u):
            return slice(PASS_WORDS * q + u, PASS_WORDS * (q + 1), 2)

        def turn_xl(i, q):
            bank = psum.tile([P, 2, N], F32, name="product", bufs=PRODUCT_BANKS)
            words = xl_rows[i][:].bitcast(F32)
            for h in range(HALVES):
                for u in range(2):
                    nc.tensor.transpose(bank[:, u, tokens(h)], words[:, h, every_second_word(q, u)], ident[:])
            dst = xl_turned[q][:, i * N * SLOTS : (i + 1) * N * SLOTS].bitcast(F32)
            nc.scalar.copy(out=dst.rearrange("p (n u) -> p n u", u=2), in_=bank[:].rearrange("p u n -> p n u"))

        def quantize_xl(q):
            nc.vector.quantize_mx(out=xl_codes[q][:].bitcast(FP8X4), scales=xl_scales[q][:], in_=xl_turned[q][:])

        def order_words(c, q):
            nc.vector.tensor_copy(
                out=w1_by_slot[c][:, q, :].rearrange("p (t a m e) -> p a t m e", t=SLOTS, m=LINE // W4, e=W4),
                in_=w1[c][:, q, :].rearrange("p (a m t e) -> p a t m e", t=SLOTS, m=LINE // W4, e=W4),
            )

        def order_scales(c):
            nc.vector.tensor_copy(
                out=s1_by_slot[c][:].rearrange("p q (t a m) -> p q a t m", t=SLOTS, m=LINE),
                in_=s1[:, :, PASS * c : PASS * (c + 1)].rearrange("p q (a m t) -> p q a t m", t=SLOTS, m=LINE),
            )

        def widen(s, parts=1):
            wide = work.tile([P, D], BF16, name="wide", bufs=3)
            for part in range(parts):
                cols = slice(part * D // parts, (part + 1) * D // parts)
                nc.vector.tensor_tensor(
                    out=wide[:, cols], in0=j_rows[s][:, cols].bitcast(FP8), in1=scale_row[:, cols], op=ALU.mult
                )
            live["wide", s] = wide

        def turn_j(s):
            bank = psum.tile([P, PASSES, 2, P], F32, name="turn", bufs=TURN_BANKS)
            words = live["wide", s][:].bitcast(F32)
            for q in range(PASSES):
                for u in range(2):
                    nc.tensor.transpose(bank[:, q, u, :], words[:, every_second_word(q, u)], ident[:])
            turned = work.tile([P, D], BF16, name="turned", bufs=3, align_bytes=64)
            nc.scalar.copy(
                out=turned[:].bitcast(F32).rearrange("p (q n u) -> p q n u", q=PASSES, u=2),
                in_=bank[:].rearrange("p q u n -> p q n u"),
            )
            live["turned", s] = turned

        def quantize_j(s):
            nc.vector.quantize_mx(out=j_codes[s][:].bitcast(FP8X4), scales=j_scales[s][:], in_=live["turned", s][:])

        def product_j(s, c):
            bank = psum.tile([P, BANK], F32, name="product", bufs=PRODUCT_BANKS)
            for q in range(PASSES):
                nc.tensor.matmul_mx(
                    out=bank[:],
                    lhsT=j_codes[s][:, q * P : (q + 1) * P].bitcast(FP8X4),
                    lhsT_scale=j_scales[s][:, q * P : (q + 1) * P],
                    rhs=w1[c][:, q, :].bitcast(FP4X4),
                    rhs_scale=s1[:, q, PASS * c : PASS * (c + 1)],
                    start=(q == 0),
                    stop=(q == PASSES - 1),
                )
            squares = work.tile([P, SLOTS, P], F32, name="squares", bufs=6)
            nc.scalar.activation(out=squares[:], in_=bank[:].rearrange("p (m t) -> p t m", t=SLOTS), func=ACT.Square)
            live["squares", s, c] = squares

        def add_pair(s, c):
            pair = work.tile([P, SLOTS, P], F32, name="pair", bufs=3)
            nc.vector.tensor_tensor(
                out=pair[:], in0=live["squares", s - 1, c][:], in1=live["squares", s, c][:], op=ALU.add
            )
            live["squares", s, c] = pair

        def fold(s, c, opens=False):
            h, k = divmod(s, K)
            if opens:
                live["sum", h, c] = psum.tile([P, SLOTS, P], F32, name="sum%d" % c)
            for t in range(SLOTS):
                nc.tensor.matmul(
                    live["sum", h, c][:, t, :],
                    lhsT=live["squares", s, c][:, t, :],
                    rhs=ident[:],
                    start=(opens and t == 0),
                    stop=(k == K - 1 and t == SLOTS - 1),
                    is_transpose=True,
                )

        def product_xl(c, t):
            bank = psum.tile([P, 2, N], F32, name="product", bufs=PRODUCT_BANKS)
            for q in range(PASSES):
                nc.tensor.matmul_mx(
                    out=bank[:].rearrange("p i n -> p (i n)"),
                    lhsT=w1_by_slot[c][:, q, W4 * P * t : W4 * P * (t + 1)].bitcast(FP4X4),
                    lhsT_scale=s1_by_slot[c][:, q, P * t : P * (t + 1)],
                    rhs=xl_codes[q][:].bitcast(FP8X4),
                    rhs_scale=xl_scales[q][:],
                    start=(q == 0),
                    stop=(q == PASSES - 1),
                )
            nc.scalar.activation(out=th[c][:, t, :], in_=bank[:, 0, :], func=ACT.Tanh, bias=bias[:, c, t : t + 1])
            nc.scalar.activation(
                out=la_gain[c][:, t, :], in_=bank[:, 1, :], func=ACT.Copy, scale=neg_gain[:, c, t : t + 1]
            )

        def apply_gain(c):
            for t in range(SLOTS):
                nc.vector.tensor_scalar(
                    out=th_gain[c][:, t, :], in0=th[c][:, t, :], scalar1=gain[:, c, t : t + 1], scalar2=None, op0=ALU.mult
                )

        def square_th(h, c):
            nc.scalar.activation(
                out=th_sq[h][c][:].rearrange("p (a i) t -> p a t i", i=4),
                in_=th[c][:, :, tokens(h)].rearrange("p t (a i) -> p a t i", i=4),
                func=ACT.Square,
            )

        def round_y(c):
            y_in = work.tile([P, N, SLOTS], BF16, name="y_in", align_bytes=64)
            nc.vector.tensor_copy(
                out=y_in[:].rearrange("p (a i) t -> p a t i", i=4), in_=th_gain[c][:].rearrange("p t (a i) -> p a t i", i=4)
            )
            live["y_in", c] = y_in

        def quantize_y(c):
            nc.vector.quantize_mx(
                out=y_codes[c][:].bitcast(FP8X4),
                scales=y_scales[c][:],
                in_=live["y_in", c][:].rearrange("p n t -> p (n t)"),
            )

        def lap_product(h, c, part=slice(0, P)):
            curve = work.tile([P, SLOTS, part.stop - part.start], F32, name="curve")
            live["curve", h, c, part.start] = curve
            nc.vector.scalar_tensor_tensor(
                out=curve[:],
                in0=live["sum", h, c][:, :, part],
                scalar=2.0,
                in1=th_gain[c][:, :, tokens(h)][:, :, part],
                op0=ALU.mult,
                op1=ALU.mult,
            )

        def lap_sum(h, c, part=slice(0, P)):
            inner = work.tile([P, SLOTS, part.stop - part.start], F32, name="inner")
            live["inner", h, c, part.start] = inner
            nc.vector.tensor_tensor(
                out=inner[:],
                in0=live["curve", h, c, part.start][:],
                in1=la_gain[c][:, :, tokens(h)][:, :, part],
                op=ALU.add,
            )

        def lap_round(h, c, part=slice(0, P)):
            if part.start == 0:
                live["lap_in", h, c] = work.tile([P, P, SLOTS], BF16, name="lap_in", align_bytes=64)
            nc.vector.scalar_tensor_tensor(
                out=live["lap_in", h, c][:, part, :],
                in0=th_sq[h][c][:, part, :],
                scalar=-1.0,
                in1=live["inner", h, c, part.start][:].rearrange("p t n -> p n t"),
                op0=ALU.add,
                op1=ALU.mult,
            )

        def lap_last(h, c):
            ranges = [slice(0, P // 2), slice(P // 2, P)]
            for step in (lap_product, lap_sum, lap_round):
                for part in ranges:
                    step(h, c, part)

        def quantize_lap(h, c):
            nc.vector.quantize_mx(
                out=lap_codes[h][c][:].bitcast(FP8X4),
                scales=lap_scales[h][c][:],
                in_=live["lap_in", h, c][:].rearrange("p n t -> p (n t)"),
            )

        def product_out(dst, h, codes, scales, last=False):
            banks = [psum.tile([P, BANK], F32, name="product", bufs=PRODUCT_BANKS) for n in range(COLS)]
            for n in range(COLS):
                for c in range(GROUPS):
                    nc.tensor.matmul_mx(
                        out=banks[n][:],
                        lhsT=codes[c].bitcast(FP8X4),
                        lhsT_scale=scales[c],
                        rhs=w2[:, c, W4 * BANK * n : W4 * BANK * (n + 1)].bitcast(FP4X4),
                        rhs_scale=s2[:, c, BANK * n : BANK * (n + 1)],
                        start=(c == 0),
                        stop=(c == GROUPS - 1),
                    )
            for n in range(COLS):
                result = work.tile([P, BANK], F32, name="result", bufs=2 * HALVES * COLS)
                if last and n == 0:
                    nc.vector.tensor_copy(out=result[:], in_=banks[n][:])
                else:
                    nc.scalar.copy(out=result[:], in_=banks[n][:])
                nc.sync.dma_start(out=dst[tokens(h), n * BANK : (n + 1) * BANK], in_=result[:])

        def product_y(h):
            product_out(out_1, h, [a[:, tokens(h)] for a in y_codes], [a[:, tokens(h)] for a in y_scales])

        def product_lap(h):
            product_out(out_0, h, [a[:] for a in lap_codes[h]], [a[:] for a in lap_scales[h]], last=(h == HALVES - 1))

        nc.vector.memset(s1[:].bitcast(I32), 0)
        nc.vector.memset(s2[:].bitcast(I32), 0)
        nc.gpsimd.memset(idle[:], 0.0)
        make_identity(nc, ident[:])

        by_slot = "(c p t) -> p c t"
        nc.sync.dma_start(out=scale_col[:], in_=j_scale.rearrange("a o (q p t) -> p (a o q) t", p=P, t=SLOTS))
        load_words(w1[0], w1_words[:, :, : W4 * PASS])
        load_j(0)
        nc.sync.dma_start(out=xl_rows[0][:], in_=x.rearrange("(h p) d -> p h d", p=P))
        load_scales(s1, w1_scales)
        load_j(1)
        nc.sync.dma_start(out=xl_rows[1][:], in_=l.rearrange("(h p) d -> p h d", p=P))
        load_j(2)
        nc.sync.dma_start(out=bias[:], in_=b.rearrange(by_slot, p=P, t=SLOTS))
        nc.sync.dma_start(out=gain[:], in_=g.rearrange(by_slot, p=P, t=SLOTS))
        load_words(w1[1], w1_words[:, :, W4 * PASS :])
        for s in range(3, J_TILES):
            load_j(s)
        load_scales(s2, w2_scales)
        load_words(w2, w2_words)

        warm_up(3)
        for q in range(PASSES):
            spread_scale(q)
        warm_up(4)
        for q in range(PASSES):
            order_words(0, q)
        widen(0, parts=PASSES)
        order_scales(0)
        widen(1)
        for q in range(PASSES):
            turn_xl(0, q)
        turn_j(0)
        warm_up(2)
        quantize_j(0)
        widen(2)
        for q in range(PASSES):
            turn_xl(1, q)
            quantize_xl(q)
        nc.vector.tensor_scalar(out=neg_gain[:], in0=gain[:], scalar1=-1.0, scalar2=None, op0=ALU.mult)
        for c in range(GROUPS):
            product_j(0, c)


        turn_j(1)
        turn_j(2)
        widen(3)
        quantize_j(1)
        order_scales(1)
        product_xl(0, 0)
        product_xl(0, 1)
        product_j(1, 0)
        product_j(1, 1)
        quantize_j(2)
        order_words(1, 0)
        order_words(1, 1)

        turn_j(3)
        add_pair(1, 0)
        widen(4)
        add_pair(1, 1)
        product_xl(0, 2)
        product_xl(0, 3)
        product_j(2, 0)
        product_j(2, 1)
        quantize_j(3)

        turn_j(4)
        fold(1, 0, opens=True)
        fold(2, 0)
        square_th(0, 0)
        widen(5)
        apply_gain(0)
        quantize_j(4)
        widen(6)
        product_xl(1, 0)
        product_j(3, 0)
        product_xl(1, 1)
        product_j(3, 1)
        round_y(0)
        widen(7)

        turn_j(5)
        turn_j(6)
        fold(3, 0)
        quantize_y(0)
        lap_product(0, 0)
        quantize_j(5)
        add_pair(3, 1)
        quantize_j(6)
        product_xl(1, 2)
        product_xl(1, 3)
        product_j(4, 0)
        product_j(5, 0)
        lap_sum(0, 0)

        turn_j(7)
        fold(1, 1, opens=True)
        fold(3, 1)
        square_th(0, 1)
        apply_gain(1)
        lap_round(0, 0)
        lap_product(0, 1)
        quantize_j(7)
        round_y(1)
        add_pair(5, 0)
        product_j(6, 0)
        product_j(4, 1)
        product_j(7, 0)
        product_j(5, 1)
        square_th(1, 0)
        quantize_y(1)
        lap_sum(0, 1)
        quantize_lap(0, 0)

        fold(5, 0, opens=True)
        fold(6, 0)
        fold(7, 0)
        lap_round(0, 1)
        add_pair(5, 1)
        lap_product(1, 0)
        quantize_lap(0, 1)
        product_j(6, 1)
        product_j(7, 1)
        square_th(1, 1)
        product_y(0)
        lap_sum(1, 0)
        lap_round(1, 0)

        fold(5, 1, opens=True)
        fold(6, 1)
        fold(7, 1)
        quantize_lap(1, 0)
        lap_last(1, 1)
        quantize_lap(1, 1)
        product_y(1)
        product_lap(0)
        product_lap(1)
